import numpy as np
import ml_dtypes


def mxq(x, axis, fmt="e4m3"):
    dtype, down = {"e4m3": (ml_dtypes.float8_e4m3fn, 7), "e5m2": (ml_dtypes.float8_e5m2, 14)}[fmt]
    v = np.moveaxis(np.asarray(x, np.float32).astype(ml_dtypes.bfloat16).astype(np.float64), axis, -1)
    blocks = v.reshape(v.shape[:-1] + (-1, 32))
    amax = np.abs(blocks).max(-1, keepdims=True)
    byte = np.maximum(np.where(amax > 0, np.frexp(amax)[1] - 1 + 127, 0) - down, 1)
    scale = np.exp2(byte - 127.0)
    codes = (blocks / scale).astype(np.float32).astype(dtype).astype(np.float64)
    return np.moveaxis((codes * scale).reshape(v.shape), -1, axis)


WIDE = False


def mx_kscale(k):
    if not WIDE:
        return np.ones(k)
    levels = np.array([10, -10, 5, -5, 0])
    if k % 512:
        return np.exp2(np.random.permutation(np.resize(levels, k // 32))).repeat(32)
    a = np.empty((k // 512, 16))
    for p in range(k // 512):
        a[p, :8] = np.random.permutation(np.resize(levels, 8))
        for g in range(8):
            far = levels[np.abs(levels - a[p, g]) >= 10]
            a[p, g + 8] = far[np.random.randint(len(far))]
    return np.exp2(a.ravel()).repeat(32)


def f64(x):
    return np.asarray(x).astype(np.float64)


def striped(idx):
    return np.tile(idx.reshape(-1, 16).T, (8, 1)).astype(np.uint16)


def unstriped(offs):
    return offs[:16].T.reshape(-1).astype(np.int64)


E2M1 = np.array([0.0, 0.5, 1.0, 1.5, 2.0, 3.0, 4.0, 6.0, -0.0, -0.5, -1.0, -1.5, -2.0, -3.0, -4.0, -6.0])


def pack_weight(w, fmt):
    k, n = w.shape
    w = f64(np.asarray(w, np.float32).astype(ml_dtypes.bfloat16)).reshape(k // 32, 32, n)
    amax = np.abs(w).max(1)
    if fmt == "e4m3":
        byte = np.frexp(amax)[1] - 1 + 127 - 7
    else:
        mant, ex = np.frexp(amax / 6.0)
        byte = np.where(mant > 0.5, ex, ex - 1) + 127
    byte = np.clip(np.where(amax > 0, byte, 1), 1, 254)
    scaled = (w * np.exp2(127.0 - byte)[:, None, :]).reshape(k, n).astype(np.float32)
    by_word = np.ascontiguousarray(scaled.reshape(k // 512, 128, 4, n).transpose(0, 1, 3, 2))
    if fmt == "e4m3":
        words = by_word.astype(ml_dtypes.float8_e4m3fn).view(np.uint8)
    else:
        c = by_word.astype(ml_dtypes.float4_e2m1fn).view(np.uint8) & 0xF
        words = (c[..., 0::2] | (c[..., 1::2] << 4)).reshape(k // 512, 128, 2 * n)
    return np.ascontiguousarray(words), np.ascontiguousarray(byte.astype(np.uint8).reshape(k // 512, 16, n))


def unpack_weight(words, scales, fmt):
    g, _, n = scales.shape
    words = np.ascontiguousarray(words).reshape(g, 128, n, -1)
    if fmt == "e4m3":
        vals = words.view(ml_dtypes.float8_e4m3fn).astype(np.float64)
    else:
        nib = np.empty((g, 128, n, 4), np.uint8)
        nib[..., 0::2] = words & 0xF
        nib[..., 1::2] = words >> 4
        vals = E2M1[nib]
    vals = vals * np.repeat(np.exp2(scales.astype(np.float64) - 127.0), 8, axis=1)[..., None]
    return vals.transpose(0, 1, 3, 2).reshape(g * 512, n)


def gelu(v):
    return 0.5 * v * (1.0 + np.tanh(np.sqrt(2.0 / np.pi) * (v + 0.044715 * v**3)))


K, H, T, S, T3, S2, P = 1536, 512, 4096, 1024, 4096, 1024, 512

def setup_inputs():
    n = np.random.standard_normal
    s = mx_kscale(K)[:, None]
    u = mx_kscale(H)[:, None]
    d = {}
    d["tab_words"], d["tab_scales"] = pack_weight(n((K, T)) * s, "e4m3")
    d["tab2_words"], d["tab2_scales"] = pack_weight(n((H, T3)) / H ** 0.5 / u, "e4m3")
    d["offs"] = striped(np.random.permutation(T)[:S])
    d["offs2"] = striped(np.random.permutation(T3)[:S2])
    d["pos1"] = striped(np.random.permutation(S)[:P])
    d["pos2"] = striped(np.random.permutation(S)[:P])
    d["w1"] = (1.2 * n((K, H)) / K ** 0.5 / s).astype(np.float32)
    d["w4_words"], d["w4_scales"] = pack_weight(1.4 * n((K, H)) / K ** 0.5 / s * u.T, "e2m1")
    d["ex"] = (0.9 * n(S)).astype(np.float32)
    d["cb"] = (0.6 * np.exp(0.4 * n(S2))).astype(np.float32)
    return d

def reference(tab_words, tab_scales, tab2_words, tab2_scales, offs, offs2, pos1, pos2, w1, w4_words, w4_scales, ex, cb):
    v = unpack_weight(tab_words, tab_scales, "e4m3")[:, unstriped(offs)]
    v2 = unpack_weight(tab2_words, tab2_scales, "e4m3")[:, unstriped(offs2)]
    w4 = unpack_weight(w4_words, w4_scales, "e2m1")
    tone = np.tanh((mxq(f64(w1), 0, "e4m3").T @ v) + f64(ex)[None, :])
    h = tone * (w4.T @ v)
    e = v2.T @ mxq(h, 0, "e4m3")
    day = e[:, unstriped(pos1)]
    lamp = e[:, unstriped(pos2)]
    return np.maximum(day, lamp) - f64(cb)[:, None] * np.minimum(day, lamp)

@@ -1,0 +1,251 @@
+from contextlib import ExitStack
+
+import concourse.mybir as mybir
+from concourse.masks import make_identity
+
+F32 = mybir.dt.float32
+BF16 = mybir.dt.bfloat16
+I32 = mybir.dt.int32
+U32 = mybir.dt.uint32
+U16 = mybir.dt.uint16
+U8 = mybir.dt.uint8
+FP8X4 = mybir.dt.float8_e4m3fn_x4
+FP4X4 = mybir.dt.float4_e2m1fn_x4
+ACT = mybir.ActivationFunctionType
+ALU = mybir.AluOpType
+
+P = 128
+K, H, T, S, S2, PAIRS = 1536, 512, 4096, 1024, 1024, 512
+PASSES = K // 512
+JT = S // P
+MT = S2 // P
+BANK = 512
+QUADS = 4
+
+FLOPS = 2 * (2 * K * H * S + H * S2 * S)
+
+
+def tile_list_iris_blank_match_kernel(
+    tc, tab_words, tab_scales, tab2_words, tab2_scales, offs, offs2, pos1, pos2,
+    w1, w4_words, w4_scales, ex, cb, out,
+):
+    nc = tc.nc
+    with ExitStack() as ctx:
+        lists = ctx.enter_context(tc.tile_pool(name="lists", bufs=1))
+        keep = ctx.enter_context(tc.tile_pool(name="keep", bufs=1))
+        ring = ctx.enter_context(tc.tile_pool(name="ring", bufs=3))
+        psum = ctx.enter_context(tc.psum_pool(name="psum", bufs=1))
+
+        def bank(b, shape):
+            return psum.tile(shape, F32, name="bank%d" % b, tag="bank%d" % b)
+
+        offs_t = lists.tile([P, S // 16], U16, name="offs_t")
+        offs2_t = lists.tile([P, S2 // 16], U16, name="offs2_t")
+        pos1_t = lists.tile([P, PAIRS // 16], U16, name="pos1_t")
+        pos2_t = lists.tile([P, PAIRS // 16], U16, name="pos2_t")
+
+        def slot(shape, dtype, name, tag):
+            return keep.tile(shape, dtype, name=name, tag=tag, align_bytes=64)
+
+        tab_w = [slot([P, T], U32, "tab_w%d" % a, "wide%d" % a) for a in range(2)]
+        tab_s = slot([P, T], U8, "tab_s", "wide2")
+        tab2_s = keep.tile([P, T], U8, name="tab2_s")
+        w4_w = keep.tile([P, PASSES, 2 * H], U8, name="w4_w", align_bytes=64)
+        w4_s = keep.tile([P, PASSES, H], U8, name="w4_s", align_bytes=64)
+        v_s = keep.tile([P, PASSES, S], U8, name="v_s", align_bytes=64)
+        v2_s = keep.tile([P, S2], U8, name="v2_s", align_bytes=64)
+        rows = keep.tile([P, P], F32, name="rows")
+        ident = keep.tile([P, P], F32, name="ident")
+
+        make_identity(nc, ident[:])
+        nc.vector.memset(rows[:], 0.0)
+        nc.vector.memset(w4_s[:].rearrange("p a n -> p (a n)").bitcast(I32), 0)
+        nc.vector.memset(tab_s[:].bitcast(I32), 0)
+        nc.vector.memset(tab2_s[:].bitcast(I32), 0)
+        nc.vector.memset(v_s[:].rearrange("p a n -> p (a n)").bitcast(I32), 0)
+        nc.vector.memset(v2_s[:].bitcast(I32), 0)
+
+        def load_words(dst, src):
+            nc.sync.dma_start(out=dst[:].bitcast(I32), in_=src.rearrange("p t i -> p (t i)").bitcast(I32))
+
+        tab_s_in = keep.tile([P, T // 4], I32, name="tab_s_in")
+        nc.sync.dma_start(offs_t[:], offs)
+        for a in range(PASSES):
+            nc.sync.dma_start(out=tab_s_in[64 + a : 112 : 3, :], in_=tab_scales[a].bitcast(I32))
+        load_words(tab_w[0], tab_words[0])
+        nc.sync.dma_start(offs2_t[:], offs2)
+        nc.sync.dma_start(pos1_t[:], pos1)
+        load_words(tab_w[1], tab_words[1])
+        nc.sync.dma_start(out=w4_w[:].bitcast(I32), in_=w4_words.rearrange("a p n -> p a n").bitcast(I32))
+        nc.sync.dma_start(pos2_t[:], pos2)
+
+        nc.gpsimd.dma_start(out=rows[0:JT, :], in_=ex.rearrange("(t p) -> t p", p=P))
+        nc.gpsimd.dma_start(out=rows[JT : JT + MT, :], in_=cb.rearrange("(t p) -> t p", p=P))
+        for q in range(QUADS):
+            nc.gpsimd.dma_start(
+                out=w4_s[32 * q : 32 * q + 4, :, :].bitcast(I32),
+                in_=w4_scales[:, 4 * q : 4 * q + 4, :].rearrange("a r n -> r a n").bitcast(I32),
+            )
+        nc.gpsimd.dma_start(out=tab2_s[0:P:8, :].bitcast(I32), in_=tab2_scales[0].bitcast(I32))
+
+        turned = bank(7, [P, P])
+        nc.tensor.transpose(turned[:], rows[:], ident[:])
+        ex_col = keep.tile([P, JT], F32, name="ex_col")
+        neg_cb = keep.tile([P, MT], F32, name="neg_cb")
+        nc.scalar.activation(out=ex_col[:], in_=turned[:, 0:JT], func=ACT.Copy)
+        nc.scalar.activation(out=neg_cb[:], in_=turned[:, JT : JT + MT], func=ACT.Copy, scale=-1.0)
+
+        v_w = [keep.tile([P, S], U32, name="v_w%d" % a, align_bytes=64) for a in range(PASSES)]
+        v_s_picked = keep.tile([P, S], U8, name="v_s_picked")
+        v2_s_picked = keep.tile([P, S2], U8, name="v2_s_picked")
+
+        nc.vector.tensor_copy(tab_s[64:112, :].bitcast(I32), tab_s_in[64:112, :])
+        nc.vector.tensor_copy(v_s_picked[:], tab_s[:].indirect(offs_t[:]))
+        for q in range(QUADS):
+            nc.sync.dma_start(
+                out=v_s[32 * q : 32 * q + 4, :, :].bitcast(I32),
+                in_=v_s_picked[64 + 12 * q : 64 + 12 * (q + 1), :].bitcast(I32),
+            )
+        tab_w.append(slot([P, T], U32, "tab_w2", "wide2"))
+        load_words(tab_w[2], tab_words[2])
+
+        nc.vector.tensor_copy(v_w[0][:], tab_w[0][:].indirect(offs_t[:]))
+        w1_raw = slot([P, PASSES, 4, H], F32, "w1_raw", "wide0")
+        for a in range(PASSES):
+            nc.sync.dma_start(
+                out=w1_raw[:, a], in_=w1[512 * a : 512 * (a + 1), :].rearrange("(p i) r -> p i r", i=4)
+            )
+        nc.vector.tensor_copy(v_w[1][:], tab_w[1][:].indirect(offs_t[:]))
+        tab2_w = slot([P, T], U32, "tab2_w", "wide1")
+        load_words(tab2_w, tab2_words[0])
+        nc.vector.tensor_copy(v2_s_picked[:], tab2_s[:].indirect(offs2_t[:]))
+        for q in range(QUADS):
+            nc.gpsimd.dma_start(
+                out=v2_s[32 * q : 32 * q + 4, :].bitcast(I32),
+                in_=v2_s_picked[32 * q : 32 * q + 32 : 8, :].bitcast(I32),
+            )
+        for c in range(2):
+            nc.vector.tensor_copy(
+                v_w[2][:, 512 * c : 512 * (c + 1)], tab_w[2][:].indirect(offs_t[:, 32 * c : 32 * (c + 1)])
+            )
+
+        def first_stage_pass(acc, t, a, words, scales):
+            cols = slice(P * t, P * (t + 1))
+            nc.tensor.matmul_mx(
+                out=acc[:], lhsT=v_w[a][:, cols].bitcast(FP8X4), lhsT_scale=v_s[:, a, cols],
+                rhs=words, rhs_scale=scales, start=(a == 0), stop=(a == PASSES - 1),
+            )
+
+        def by_pairs(acc):
+            return acc[:].rearrange("p (q u e) -> p u q e", u=2, e=2)
+
+        def as_pairs(tile):
+            return tile[:].rearrange("p (u q e) -> p u q e", u=2, e=2)
+
+        acc4 = [bank(t, [P, BANK]) for t in range(JT)]
+        for t in range(JT):
+            for a in range(PASSES):
+                first_stage_pass(acc4[t], t, a, w4_w[:, a, :].bitcast(FP4X4), w4_s[:, a, :])
+        second = [slot([P, H], F32, "second%d" % t, "second%d" % t) for t in range(JT)]
+        for t in range(JT):
+            nc.scalar.copy(out=as_pairs(second[t]), in_=by_pairs(acc4[t]))
+
+        w1_w = [keep.tile([P, H], U32, name="w1_w%d" % a, align_bytes=64) for a in range(PASSES)]
+        w1_s = [keep.tile([P, H], U8, name="w1_s%d" % a, align_bytes=64) for a in range(PASSES)]
+        acc1 = [bank(t, [P, BANK]) for t in range(JT)]
+        w1_bf = slot([P, PASSES, 4 * H], BF16, "w1_bf", "wide2")
+        for a in range(PASSES):
+            nc.vector.tensor_copy(
+                out=w1_bf[:, a, :].rearrange("p (c n i) -> p c i n", n=4, i=4),
+                in_=w1_raw[:, a].rearrange("p i (c n) -> p c i n", n=4),
+            )
+            nc.vector.quantize_mx(out=w1_w[a][:].bitcast(FP8X4), scales=w1_s[a][:], in_=w1_bf[:, a, :])
+        for t in range(JT):
+            for a in range(PASSES):
+                first_stage_pass(acc1[t], t, a, w1_w[a][:].bitcast(FP8X4), w1_s[a][:])
+
+        h_w = keep.tile([P, S], U32, name="h_w", align_bytes=64)
+        h_s = keep.tile([P, S], U8, name="h_s", align_bytes=64)
+
+        def make_h(t):
+            tone = ring.tile([P, H], F32, name="tone")
+            nc.scalar.activation(
+                out=as_pairs(tone), in_=by_pairs(acc1[t]), func=ACT.Tanh, bias=ex_col[:, t : t + 1]
+            )
+            h_t = ring.tile([P, H], BF16, name="h_t", bufs=4)
+            nc.vector.tensor_tensor(h_t[:], tone[:], second[t][:], ALU.mult)
+            return h_t
+
+        def turn_and_quantise(g, h_pair):
+            xt = bank(g, [P, 2, 2, P])
+            for t in range(2):
+                words = h_pair[t][:].bitcast(F32)
+                for u in range(2):
+                    nc.tensor.transpose(xt[:, t, u, :], words[:, P * u : P * (u + 1)], ident[:])
+            h_bf = ring.tile([P, 4 * 2 * P], BF16, name="h_bf", align_bytes=64)
+            nc.scalar.copy(
+                out=h_bf[:].bitcast(F32).rearrange("p (t j u) -> p t j u", t=2, u=2),
+                in_=xt[:].rearrange("p t u j -> p t j u"),
+            )
+            cols = slice(2 * P * g, 2 * P * (g + 1))
+            nc.vector.quantize_mx(out=h_w[:, cols].bitcast(FP8X4), scales=h_s[:, cols], in_=h_bf[:])
+
+        def gather_candidates(c, after):
+            half = slot([P, S2 // 2], U32, "v2_w%d" % c, "second%d" % after)
+            nc.vector.tensor_copy(half[:], tab2_w[:].indirect(offs2_t[:, 32 * c : 32 * (c + 1)]))
+            return half
+
+        v2_w = []
+        h_tiles = [make_h(0), make_h(1)]
+        for g in range(JT // 2):
+            if g == 1:
+                v2_w.append(gather_candidates(0, 3))
+            if g == 3:
+                v2_w.append(gather_candidates(1, 7))
+            if g + 1 < JT // 2:
+                h_tiles.extend([make_h(2 * g + 2), make_h(2 * g + 3)])
+            turn_and_quantise(g, h_tiles[2 * g : 2 * g + 2])
+
+        def scores(m):
+            e = ring.tile([P, S], F32, name="e")
+            rows_m = slice(P * m, P * (m + 1))
+            for c in range(2):
+                cols = slice(BANK * c, BANK * (c + 1))
+                acc = bank((4 + 2 * m + c) % 8, [P, BANK])
+                nc.tensor.matmul_mx(
+                    out=acc[:], lhsT=v2_w[m // 4][:, P * (m % 4) : P * (m % 4 + 1)].bitcast(FP8X4), lhsT_scale=v2_s[:, rows_m],
+                    rhs=h_w[:, cols].bitcast(FP8X4), rhs_scale=h_s[:, cols], start=True, stop=True,
+                )
+                nc.scalar.copy(out=e[:, cols], in_=acc[:])
+            return e
+
+        def pick(e, positions, name):
+            picked = ring.tile([P, PAIRS], F32, name=name)
+            nc.vector.tensor_copy(picked[:], e[:].indirect(positions[:]))
+            return picked
+
+        def larger_smaller(day, lamp):
+            larger = ring.tile([P, PAIRS], F32, name="larger", bufs=2)
+            smaller = ring.tile([P, PAIRS], F32, name="smaller", bufs=2)
+            nc.vector.tensor_tensor(larger[:], day[:], lamp[:], ALU.max)
+            nc.vector.tensor_tensor(smaller[:], day[:], lamp[:], ALU.min)
+            return larger, smaller
+
+        def finish(m, larger, smaller):
+            result = ring.tile([P, PAIRS], F32, name="result")
+            nc.vector.scalar_tensor_tensor(
+                result[:], smaller[:], neg_cb[:, m : m + 1], larger[:], ALU.mult, ALU.add
+            )
+            nc.sync.dma_start(out=out[P * m : P * (m + 1), :], in_=result[:])
+
+        e = scores(0)
+        day = pick(e, pos1_t, "day")
+        lamp = pick(e, pos2_t, "lamp")
+        for m in range(1, MT):
+            e = scores(m)
+            next_day = pick(e, pos1_t, "day")
+            both = larger_smaller(day, lamp)
+            next_lamp = pick(e, pos2_t, "lamp")
+            finish(m - 1, *both)
+            day, lamp = next_day, next_lamp
+        finish(MT - 1, *larger_smaller(day, lamp))

@@ -21,6 +21,8 @@ JT = S // P
 MT = S2 // P
 BANK = 512
 QUADS = 4
+E_SLOTS = 4
+LAMP_SLOTS = 4
 
 FLOPS = 2 * (2 * K * H * S + H * S2 * S)
 
@@ -33,6 +35,7 @@ def tile_list_iris_blank_match_kernel(
     with ExitStack() as ctx:
         lists = ctx.enter_context(tc.tile_pool(name="lists", bufs=1))
         keep = ctx.enter_context(tc.tile_pool(name="keep", bufs=1))
+        shared = ctx.enter_context(tc.tile_pool(name="shared", bufs=1))
         ring = ctx.enter_context(tc.tile_pool(name="ring", bufs=3))
         psum = ctx.enter_context(tc.psum_pool(name="psum", bufs=1))
 
@@ -47,7 +50,7 @@ def tile_list_iris_blank_match_kernel(
         def slot(shape, dtype, name, tag):
             return keep.tile(shape, dtype, name=name, tag=tag, align_bytes=64)
 
-        tab_w = [slot([P, T], U32, "tab_w%d" % a, "wide%d" % a) for a in range(2)]
+        tab_w = [shared.tile([P, T], U32, name="tab_w0", offset=4096), slot([P, T], U32, "tab_w1", "wide1")]
         tab_s = slot([P, T], U8, "tab_s", "wide2")
         tab2_s = keep.tile([P, T], U8, name="tab2_s")
         w4_w = keep.tile([P, PASSES, 2 * H], U8, name="w4_w", align_bytes=64)
@@ -57,9 +60,8 @@ def tile_list_iris_blank_match_kernel(
         rows = keep.tile([P, P], F32, name="rows")
         ident = keep.tile([P, P], F32, name="ident")
 
-        make_identity(nc, ident[:])
-        nc.vector.memset(rows[:], 0.0)
         nc.vector.memset(w4_s[:].rearrange("p a n -> p (a n)").bitcast(I32), 0)
+        nc.vector.memset(rows[:], 0.0)
         nc.vector.memset(tab_s[:].bitcast(I32), 0)
         nc.vector.memset(tab2_s[:].bitcast(I32), 0)
         nc.vector.memset(v_s[:].rearrange("p a n -> p (a n)").bitcast(I32), 0)
@@ -75,25 +77,21 @@ def tile_list_iris_blank_match_kernel(
         load_words(tab_w[0], tab_words[0])
         nc.sync.dma_start(offs2_t[:], offs2)
         nc.sync.dma_start(pos1_t[:], pos1)
+        tab2_s_in = keep.tile([P, T // 4], I32, name="tab2_s_in")
+        nc.sync.dma_start(out=tab2_s_in[0:16, :], in_=tab2_scales[0].bitcast(I32))
         load_words(tab_w[1], tab_words[1])
         nc.sync.dma_start(out=w4_w[:].bitcast(I32), in_=w4_words.rearrange("a p n -> p a n").bitcast(I32))
         nc.sync.dma_start(pos2_t[:], pos2)
 
-        nc.gpsimd.dma_start(out=rows[0:JT, :], in_=ex.rearrange("(t p) -> t p", p=P))
-        nc.gpsimd.dma_start(out=rows[JT : JT + MT, :], in_=cb.rearrange("(t p) -> t p", p=P))
         for q in range(QUADS):
             nc.gpsimd.dma_start(
                 out=w4_s[32 * q : 32 * q + 4, :, :].bitcast(I32),
                 in_=w4_scales[:, 4 * q : 4 * q + 4, :].rearrange("a r n -> r a n").bitcast(I32),
             )
-        nc.gpsimd.dma_start(out=tab2_s[0:P:8, :].bitcast(I32), in_=tab2_scales[0].bitcast(I32))
+        nc.gpsimd.dma_start(out=rows[0:JT, :], in_=ex.rearrange("(t p) -> t p", p=P))
+        nc.gpsimd.dma_start(out=rows[JT : JT + MT, :], in_=cb.rearrange("(t p) -> t p", p=P))
 
-        turned = bank(7, [P, P])
-        nc.tensor.transpose(turned[:], rows[:], ident[:])
-        ex_col = keep.tile([P, JT], F32, name="ex_col")
-        neg_cb = keep.tile([P, MT], F32, name="neg_cb")
-        nc.scalar.activation(out=ex_col[:], in_=turned[:, 0:JT], func=ACT.Copy)
-        nc.scalar.activation(out=neg_cb[:], in_=turned[:, JT : JT + MT], func=ACT.Copy, scale=-1.0)
+        make_identity(nc, ident[:])
 
         v_w = [keep.tile([P, S], U32, name="v_w%d" % a, align_bytes=64) for a in range(PASSES)]
         v_s_picked = keep.tile([P, S], U8, name="v_s_picked")
@@ -110,20 +108,21 @@ def tile_list_iris_blank_match_kernel(
         load_words(tab_w[2], tab_words[2])
 
         nc.vector.tensor_copy(v_w[0][:], tab_w[0][:].indirect(offs_t[:]))
-        w1_raw = slot([P, PASSES, 4, H], F32, "w1_raw", "wide0")
+        w1_raw = [shared.tile([P, 4, H], F32, name="w1_raw%d" % a, offset=8192 * a) for a in range(PASSES)]
         for a in range(PASSES):
             nc.sync.dma_start(
-                out=w1_raw[:, a], in_=w1[512 * a : 512 * (a + 1), :].rearrange("(p i) r -> p i r", i=4)
+                out=w1_raw[a][:], in_=w1[512 * a : 512 * (a + 1), :].rearrange("(p i) r -> p i r", i=4)
             )
-        nc.vector.tensor_copy(v_w[1][:], tab_w[1][:].indirect(offs_t[:]))
-        tab2_w = slot([P, T], U32, "tab2_w", "wide1")
-        load_words(tab2_w, tab2_words[0])
+        nc.vector.tensor_copy(tab2_s[0:16, :].bitcast(I32), tab2_s_in[0:16, :])
         nc.vector.tensor_copy(v2_s_picked[:], tab2_s[:].indirect(offs2_t[:]))
         for q in range(QUADS):
             nc.gpsimd.dma_start(
                 out=v2_s[32 * q : 32 * q + 4, :].bitcast(I32),
-                in_=v2_s_picked[32 * q : 32 * q + 32 : 8, :].bitcast(I32),
+                in_=v2_s_picked[4 * q : 4 * q + 4, :].bitcast(I32),
             )
+        nc.vector.tensor_copy(v_w[1][:], tab_w[1][:].indirect(offs_t[:]))
+        tab2_w = slot([P, T], U32, "tab2_w", "wide1")
+        load_words(tab2_w, tab2_words[0])
         for c in range(2):
             nc.vector.tensor_copy(
                 v_w[2][:, 512 * c : 512 * (c + 1)], tab_w[2][:].indirect(offs_t[:, 32 * c : 32 * (c + 1)])
@@ -150,15 +149,23 @@ def tile_list_iris_blank_match_kernel(
         for t in range(JT):
             nc.scalar.copy(out=as_pairs(second[t]), in_=by_pairs(acc4[t]))
 
+        turned = bank(0, [P, P])
+        nc.tensor.transpose(turned[:], rows[:], ident[:])
+        ex_col = keep.tile([P, JT], F32, name="ex_col")
+        neg_cb = keep.tile([P, MT], F32, name="neg_cb")
+        nc.scalar.activation(out=ex_col[:], in_=turned[:, 0:JT], func=ACT.Copy)
+        nc.scalar.activation(out=neg_cb[:], in_=turned[:, JT : JT + MT], func=ACT.Copy, scale=-1.0)
+        one_cb = keep.tile([P, MT], F32, name="one_cb")
+        nc.scalar.activation(out=one_cb[:], in_=turned[:, JT : JT + MT], func=ACT.Copy, bias=1.0)
+
         w1_w = [keep.tile([P, H], U32, name="w1_w%d" % a, align_bytes=64) for a in range(PASSES)]
         w1_s = [keep.tile([P, H], U8, name="w1_s%d" % a, align_bytes=64) for a in range(PASSES)]
         acc1 = [bank(t, [P, BANK]) for t in range(JT)]
         w1_bf = slot([P, PASSES, 4 * H], BF16, "w1_bf", "wide2")
         for a in range(PASSES):
-            nc.vector.tensor_copy(
-                out=w1_bf[:, a, :].rearrange("p (c n i) -> p c i n", n=4, i=4),
-                in_=w1_raw[:, a].rearrange("p i (c n) -> p c i n", n=4),
-            )
+            woven = w1_bf[:, a, :].rearrange("p (c n i) -> p c i n", n=4, i=4)
+            plain = w1_raw[a][:].rearrange("p i (c n) -> p c i n", n=4)
+            nc.vector.tensor_copy(out=woven, in_=plain)
             nc.vector.quantize_mx(out=w1_w[a][:].bitcast(FP8X4), scales=w1_s[a][:], in_=w1_bf[:, a, :])
         for t in range(JT):
             for a in range(PASSES):
@@ -190,8 +197,8 @@ def tile_list_iris_blank_match_kernel(
             cols = slice(2 * P * g, 2 * P * (g + 1))
             nc.vector.quantize_mx(out=h_w[:, cols].bitcast(FP8X4), scales=h_s[:, cols], in_=h_bf[:])
 
-        def gather_candidates(c, after):
-            half = slot([P, S2 // 2], U32, "v2_w%d" % c, "second%d" % after)
+        def gather_candidates(c, tag):
+            half = slot([P, S2 // 2], U32, "v2_w%d" % c, tag)
             nc.vector.tensor_copy(half[:], tab2_w[:].indirect(offs2_t[:, 32 * c : 32 * (c + 1)]))
             return half
 
@@ -199,19 +206,20 @@ def tile_list_iris_blank_match_kernel(
         h_tiles = [make_h(0), make_h(1)]
         for g in range(JT // 2):
             if g == 1:
-                v2_w.append(gather_candidates(0, 3))
+                v2_w.append(gather_candidates(0, "second2"))
             if g == 3:
-                v2_w.append(gather_candidates(1, 7))
+                v2_w.append(gather_candidates(1, "second7"))
             if g + 1 < JT // 2:
                 h_tiles.extend([make_h(2 * g + 2), make_h(2 * g + 3)])
             turn_and_quantise(g, h_tiles[2 * g : 2 * g + 2])
 
         def scores(m):
-            e = ring.tile([P, S], F32, name="e")
+            e = slot([P, S], F32, "e", "e%d" % (m % E_SLOTS))
             rows_m = slice(P * m, P * (m + 1))
             for c in range(2):
                 cols = slice(BANK * c, BANK * (c + 1))
-                acc = bank((4 + 2 * m + c) % 8, [P, BANK])
+                step = 2 * m + c
+                acc = bank(4 if step == 0 else (5, 3, 6)[(step - 1) % 3], [P, BANK])
                 nc.tensor.matmul_mx(
                     out=acc[:], lhsT=v2_w[m // 4][:, P * (m % 4) : P * (m % 4 + 1)].bitcast(FP8X4), lhsT_scale=v2_s[:, rows_m],
                     rhs=h_w[:, cols].bitcast(FP8X4), rhs_scale=h_s[:, cols], start=True, stop=True,
@@ -219,33 +227,50 @@ def tile_list_iris_blank_match_kernel(
                 nc.scalar.copy(out=e[:, cols], in_=acc[:])
             return e
 
-        def pick(e, positions, name):
-            picked = ring.tile([P, PAIRS], F32, name=name)
+        def pick(e, positions, picked):
             nc.vector.tensor_copy(picked[:], e[:].indirect(positions[:]))
             return picked
 
-        def larger_smaller(day, lamp):
-            larger = ring.tile([P, PAIRS], F32, name="larger", bufs=2)
-            smaller = ring.tile([P, PAIRS], F32, name="smaller", bufs=2)
-            nc.vector.tensor_tensor(larger[:], day[:], lamp[:], ALU.max)
-            nc.vector.tensor_tensor(smaller[:], day[:], lamp[:], ALU.min)
-            return larger, smaller
+        def lamp_slot(m, name):
+            return slot([P, PAIRS], F32, name, "lamp%d" % (m % LAMP_SLOTS))
 
-        def finish(m, larger, smaller):
-            result = ring.tile([P, PAIRS], F32, name="result")
+        def base_and_gap(m, day, lamp):
+            base = ring.tile([P, PAIRS], F32, name="base")
+            nc.vector.scalar_tensor_tensor(base[:], lamp[:], neg_cb[:, m : m + 1], day[:], ALU.mult, ALU.add)
+            gap = ring.tile([P, PAIRS], F32, name="gap", bufs=3)
+            nc.gpsimd.tensor_tensor(gap[:], lamp[:], day[:], ALU.subtract)
+            return base, gap
+
+        def finish(m, base, gap):
+            above = slot([P, PAIRS], F32, "above", "e%d" % ((m + 1) % E_SLOTS))
+            nc.scalar.activation(out=above[:], in_=gap[:], func=ACT.Relu)
+            scaled = ring.tile([P, PAIRS], F32, name="scaled", bufs=2)
+            nc.scalar.activation(out=scaled[:], in_=above[:], func=ACT.Copy, scale=one_cb[:, m : m + 1])
+            result = lamp_slot(m + 1, "result")
+            nc.gpsimd.tensor_tensor(result[:], base[:], scaled[:], ALU.add)
+            nc.sync.dma_start(out=out[P * m : P * (m + 1), :], in_=result[:])
+
+        def finish_on_vector(m, day, lamp):
+            larger = ring.tile([P, PAIRS], F32, name="larger", bufs=1)
+            smaller = ring.tile([P, PAIRS], F32, name="smaller", bufs=1)
+            nc.vector.tensor_tensor(smaller[:], day[:], lamp[:], ALU.min)
+            nc.vector.tensor_tensor(larger[:], day[:], lamp[:], ALU.max)
+            result = ring.tile([P, PAIRS], F32, name="last_result", bufs=1)
             nc.vector.scalar_tensor_tensor(
                 result[:], smaller[:], neg_cb[:, m : m + 1], larger[:], ALU.mult, ALU.add
             )
             nc.sync.dma_start(out=out[P * m : P * (m + 1), :], in_=result[:])
 
-        e = scores(0)
-        day = pick(e, pos1_t, "day")
-        lamp = pick(e, pos2_t, "lamp")
-        for m in range(1, MT):
+        parts = []
+        for m in range(MT - 1):
             e = scores(m)
-            next_day = pick(e, pos1_t, "day")
-            both = larger_smaller(day, lamp)
-            next_lamp = pick(e, pos2_t, "lamp")
-            finish(m - 1, *both)
-            day, lamp = next_day, next_lamp
-        finish(MT - 1, *larger_smaller(day, lamp))
+            day = pick(e, pos1_t, ring.tile([P, PAIRS], F32, name="day", bufs=3))
+            lamp = pick(e, pos2_t, lamp_slot(m, "lamp"))
+            parts.append(base_and_gap(m, day, lamp))
+            if m > 0:
+                finish(m - 1, *parts[m - 1])
+        e = scores(MT - 1)
+        day = pick(e, pos1_t, ring.tile([P, PAIRS], F32, name="day", bufs=3))
+        lamp = pick(e, pos2_t, ring.tile([P, PAIRS], F32, name="last_lamp", bufs=1))
+        finish(MT - 2, *parts[MT - 2])
+        finish_on_vector(MT - 1, day, lamp)

@@ -21,6 +21,7 @@ JT = S // P
 MT = S2 // P
 BANK = 512
 QUADS = 4
+COPIED = 6
 E_SLOTS = 4
 LAMP_SLOTS = 4
 
@@ -50,7 +51,7 @@ def tile_list_iris_blank_match_kernel(
         def slot(shape, dtype, name, tag):
             return keep.tile(shape, dtype, name=name, tag=tag, align_bytes=64)
 
-        tab_w = [shared.tile([P, T], U32, name="tab_w0", offset=4096), slot([P, T], U32, "tab_w1", "wide1")]
+        tab_w = [shared.tile([P, T], U32, name="tab_w0", offset=6144), slot([P, T], U32, "tab_w1", "wide1")]
         tab_s = slot([P, T], U8, "tab_s", "wide2")
         tab2_s = keep.tile([P, T], U8, name="tab2_s")
         w4_w = keep.tile([P, PASSES, 2 * H], U8, name="w4_w", align_bytes=64)
@@ -108,11 +109,14 @@ def tile_list_iris_blank_match_kernel(
         load_words(tab_w[2], tab_words[2])
 
         nc.vector.tensor_copy(v_w[0][:], tab_w[0][:].indirect(offs_t[:]))
-        w1_raw = [shared.tile([P, 4, H], F32, name="w1_raw%d" % a, offset=8192 * a) for a in range(PASSES)]
-        for a in range(PASSES):
+        w1_pieces = [(0, 0, H), (1, 0, H), (2, 0, H // 2), (2, H // 2, H)]
+        w1_raw = []
+        for n, (a, lo, hi) in enumerate(w1_pieces):
+            piece = shared.tile([P, 4, hi - lo], F32, name="w1_raw%d" % n, offset=16 * (a * H + lo))
             nc.sync.dma_start(
-                out=w1_raw[a][:], in_=w1[512 * a : 512 * (a + 1), :].rearrange("(p i) r -> p i r", i=4)
+                out=piece[:], in_=w1[512 * a : 512 * (a + 1), lo:hi].rearrange("(p i) r -> p i r", i=4)
             )
+            w1_raw.append(piece)
         nc.vector.tensor_copy(tab2_s[0:16, :].bitcast(I32), tab2_s_in[0:16, :])
         nc.vector.tensor_copy(v2_s_picked[:], tab2_s[:].indirect(offs2_t[:]))
         for q in range(QUADS):
@@ -123,9 +127,9 @@ def tile_list_iris_blank_match_kernel(
         nc.vector.tensor_copy(v_w[1][:], tab_w[1][:].indirect(offs_t[:]))
         tab2_w = slot([P, T], U32, "tab2_w", "wide1")
         load_words(tab2_w, tab2_words[0])
-        for c in range(2):
+        for c in range(4):
             nc.vector.tensor_copy(
-                v_w[2][:, 512 * c : 512 * (c + 1)], tab_w[2][:].indirect(offs_t[:, 32 * c : 32 * (c + 1)])
+                v_w[2][:, 256 * c : 256 * (c + 1)], tab_w[2][:].indirect(offs_t[:, 16 * c : 16 * (c + 1)])
             )
 
         def first_stage_pass(acc, t, a, words, scales):
@@ -145,46 +149,59 @@ def tile_list_iris_blank_match_kernel(
         for t in range(JT):
             for a in range(PASSES):
                 first_stage_pass(acc4[t], t, a, w4_w[:, a, :].bitcast(FP4X4), w4_s[:, a, :])
-        second = [slot([P, H], F32, "second%d" % t, "second%d" % t) for t in range(JT)]
-        for t in range(JT):
+        second = [slot([P, H], F32, "second%d" % t, "second%d" % t) for t in range(COPIED)]
+        for t in range(COPIED):
             nc.scalar.copy(out=as_pairs(second[t]), in_=by_pairs(acc4[t]))
 
         turned = bank(0, [P, P])
         nc.tensor.transpose(turned[:], rows[:], ident[:])
-        ex_col = keep.tile([P, JT], F32, name="ex_col")
-        neg_cb = keep.tile([P, MT], F32, name="neg_cb")
-        nc.scalar.activation(out=ex_col[:], in_=turned[:, 0:JT], func=ACT.Copy)
-        nc.scalar.activation(out=neg_cb[:], in_=turned[:, JT : JT + MT], func=ACT.Copy, scale=-1.0)
-        one_cb = keep.tile([P, MT], F32, name="one_cb")
-        nc.scalar.activation(out=one_cb[:], in_=turned[:, JT : JT + MT], func=ACT.Copy, bias=1.0)
+        columns = keep.tile([P, JT + MT], F32, name="columns")
+        nc.scalar.copy(out=columns[:], in_=turned[:, 0 : JT + MT])
+
+        def from_cb(name, factor, shift):
+            made = keep.tile([P, MT], F32, name=name)
+            nc.gpsimd.tensor_scalar(made[:], columns[:, JT : JT + MT], factor, shift, ALU.mult, ALU.add)
+            return made
+
+        neg_cb = from_cb("neg_cb", -1.0, 0.0)
+        one_cb = from_cb("one_cb", 1.0, 1.0)
+        one_minus_cb = from_cb("one_minus_cb", -1.0, 1.0)
 
         w1_w = [keep.tile([P, H], U32, name="w1_w%d" % a, align_bytes=64) for a in range(PASSES)]
         w1_s = [keep.tile([P, H], U8, name="w1_s%d" % a, align_bytes=64) for a in range(PASSES)]
-        acc1 = [bank(t, [P, BANK]) for t in range(JT)]
         w1_bf = slot([P, PASSES, 4 * H], BF16, "w1_bf", "wide2")
-        for a in range(PASSES):
-            woven = w1_bf[:, a, :].rearrange("p (c n i) -> p c i n", n=4, i=4)
-            plain = w1_raw[a][:].rearrange("p i (c n) -> p c i n", n=4)
-            nc.vector.tensor_copy(out=woven, in_=plain)
-            nc.vector.quantize_mx(out=w1_w[a][:].bitcast(FP8X4), scales=w1_s[a][:], in_=w1_bf[:, a, :])
-        for t in range(JT):
+        for piece, (a, lo, hi) in zip(w1_raw, w1_pieces):
+            rounded = w1_bf[:, a, 4 * lo : 4 * hi]
+            nc.vector.tensor_copy(
+                out=rounded.rearrange("p (c n i) -> p c i n", n=4, i=4),
+                in_=piece[:].rearrange("p i (c n) -> p c i n", n=4),
+            )
+            nc.vector.quantize_mx(out=w1_w[a][:, lo:hi].bitcast(FP8X4), scales=w1_s[a][:, lo:hi], in_=rounded)
+
+        def first_product(t):
+            acc = bank(t % COPIED, [P, BANK])
             for a in range(PASSES):
-                first_stage_pass(acc1[t], t, a, w1_w[a][:].bitcast(FP8X4), w1_s[a][:])
+                first_stage_pass(acc, t, a, w1_w[a][:].bitcast(FP8X4), w1_s[a][:])
+            return acc
+
+        acc1 = [first_product(t) for t in range(COPIED)]
 
         h_w = keep.tile([P, S], U32, name="h_w", align_bytes=64)
         h_s = keep.tile([P, S], U8, name="h_s", align_bytes=64)
 
         def make_h(t):
-            tone = ring.tile([P, H], F32, name="tone")
-            nc.scalar.activation(
-                out=as_pairs(tone), in_=by_pairs(acc1[t]), func=ACT.Tanh, bias=ex_col[:, t : t + 1]
-            )
+            acc = acc1[t] if t < COPIED else first_product(t)
+            tone = slot([P, H], F32, "tone", "tone%d" % t)
+            nc.scalar.activation(out=as_pairs(tone), in_=by_pairs(acc), func=ACT.Tanh, bias=columns[:, t : t + 1])
             h_t = ring.tile([P, H], BF16, name="h_t", bufs=4)
-            nc.vector.tensor_tensor(h_t[:], tone[:], second[t][:], ALU.mult)
+            if t < COPIED:
+                nc.vector.tensor_tensor(h_t[:], tone[:], second[t][:], ALU.mult)
+            else:
+                nc.vector.tensor_tensor(as_pairs(h_t), as_pairs(tone), by_pairs(acc4[t]), ALU.mult)
             return h_t
 
         def turn_and_quantise(g, h_pair):
-            xt = bank(g, [P, 2, 2, P])
+            xt = bank(2 + g, [P, 2, 2, P])
             for t in range(2):
                 words = h_pair[t][:].bitcast(F32)
                 for u in range(2):
@@ -206,9 +223,9 @@ def tile_list_iris_blank_match_kernel(
         h_tiles = [make_h(0), make_h(1)]
         for g in range(JT // 2):
             if g == 1:
-                v2_w.append(gather_candidates(0, "second2"))
+                v2_w.append(gather_candidates(0, "tone1"))
             if g == 3:
-                v2_w.append(gather_candidates(1, "second7"))
+                v2_w.append(gather_candidates(1, "tone7"))
             if g + 1 < JT // 2:
                 h_tiles.extend([make_h(2 * g + 2), make_h(2 * g + 3)])
             turn_and_quantise(g, h_tiles[2 * g : 2 * g + 2])
@@ -216,10 +233,10 @@ def tile_list_iris_blank_match_kernel(
         def scores(m):
             e = slot([P, S], F32, "e", "e%d" % (m % E_SLOTS))
             rows_m = slice(P * m, P * (m + 1))
-            for c in range(2):
-                cols = slice(BANK * c, BANK * (c + 1))
-                step = 2 * m + c
-                acc = bank(4 if step == 0 else (5, 3, 6)[(step - 1) % 3], [P, BANK])
+            width = BANK // 2 if m == 0 else BANK
+            for c in range(S // width):
+                cols = slice(width * c, width * (c + 1))
+                acc = bank(2 + c if m == 0 else (5, 0)[c], [P, width])
                 nc.tensor.matmul_mx(
                     out=acc[:], lhsT=v2_w[m // 4][:, P * (m % 4) : P * (m % 4 + 1)].bitcast(FP8X4), lhsT_scale=v2_s[:, rows_m],
                     rhs=h_w[:, cols].bitcast(FP8X4), rhs_scale=h_s[:, cols], start=True, stop=True,
@@ -227,50 +244,28 @@ def tile_list_iris_blank_match_kernel(
                 nc.scalar.copy(out=e[:, cols], in_=acc[:])
             return e
 
-        def pick(e, positions, picked):
-            nc.vector.tensor_copy(picked[:], e[:].indirect(positions[:]))
-            return picked
-
-        def lamp_slot(m, name):
-            return slot([P, PAIRS], F32, name, "lamp%d" % (m % LAMP_SLOTS))
-
-        def base_and_gap(m, day, lamp):
-            base = ring.tile([P, PAIRS], F32, name="base")
-            nc.vector.scalar_tensor_tensor(base[:], lamp[:], neg_cb[:, m : m + 1], day[:], ALU.mult, ALU.add)
-            gap = ring.tile([P, PAIRS], F32, name="gap", bufs=3)
-            nc.gpsimd.tensor_tensor(gap[:], lamp[:], day[:], ALU.subtract)
-            return base, gap
-
-        def finish(m, base, gap):
-            above = slot([P, PAIRS], F32, "above", "e%d" % ((m + 1) % E_SLOTS))
+        def pick_pairs(m, e):
+            day = ring.tile([P, PAIRS], F32, name="day")
+            nc.vector.tensor_copy(day[:], e[:].indirect(pos1_t[:]))
+            gap = ring.tile([P, PAIRS], F32, name="gap")
+            nc.vector.tensor_tensor(gap[:], e[:].indirect(pos2_t[:]), day[:], ALU.subtract)
+            day_part = ring.tile([P, PAIRS], F32, name="day_part")
+            nc.scalar.activation(out=day_part[:], in_=day[:], func=ACT.Copy, scale=one_minus_cb[:, m : m + 1])
+            above = ring.tile([P, PAIRS], F32, name="above")
             nc.scalar.activation(out=above[:], in_=gap[:], func=ACT.Relu)
-            scaled = ring.tile([P, PAIRS], F32, name="scaled", bufs=2)
-            nc.scalar.activation(out=scaled[:], in_=above[:], func=ACT.Copy, scale=one_cb[:, m : m + 1])
-            result = lamp_slot(m + 1, "result")
-            nc.gpsimd.tensor_tensor(result[:], base[:], scaled[:], ALU.add)
-            nc.sync.dma_start(out=out[P * m : P * (m + 1), :], in_=result[:])
+            return gap, day_part, above
 
-        def finish_on_vector(m, day, lamp):
-            larger = ring.tile([P, PAIRS], F32, name="larger", bufs=1)
-            smaller = ring.tile([P, PAIRS], F32, name="smaller", bufs=1)
-            nc.vector.tensor_tensor(smaller[:], day[:], lamp[:], ALU.min)
-            nc.vector.tensor_tensor(larger[:], day[:], lamp[:], ALU.max)
-            result = ring.tile([P, PAIRS], F32, name="last_result", bufs=1)
-            nc.vector.scalar_tensor_tensor(
-                result[:], smaller[:], neg_cb[:, m : m + 1], larger[:], ALU.mult, ALU.add
-            )
-            nc.sync.dma_start(out=out[P * m : P * (m + 1), :], in_=result[:])
+        def finish(m, gap, day_part, above):
+            linear = ring.tile([P, PAIRS], F32, name="linear", bufs=2)
+            nc.vector.scalar_tensor_tensor(linear[:], gap[:], neg_cb[:, m : m + 1], day_part[:], ALU.mult, ALU.add)
+            result = ring.tile([P, PAIRS], F32, name="result")
+            width = PAIRS // 2 if m == MT - 1 else PAIRS
+            for lo in range(0, PAIRS, width):
+                cols = slice(lo, lo + width)
+                nc.vector.scalar_tensor_tensor(
+                    result[:, cols], above[:, cols], one_cb[:, m : m + 1], linear[:, cols], ALU.mult, ALU.add
+                )
+                nc.sync.dma_start(out=out[P * m : P * (m + 1), cols], in_=result[:, cols])
 
-        parts = []
-        for m in range(MT - 1):
-            e = scores(m)
-            day = pick(e, pos1_t, ring.tile([P, PAIRS], F32, name="day", bufs=3))
-            lamp = pick(e, pos2_t, lamp_slot(m, "lamp"))
-            parts.append(base_and_gap(m, day, lamp))
-            if m > 0:
-                finish(m - 1, *parts[m - 1])
-        e = scores(MT - 1)
-        day = pick(e, pos1_t, ring.tile([P, PAIRS], F32, name="day", bufs=3))
-        lamp = pick(e, pos2_t, ring.tile([P, PAIRS], F32, name="last_lamp", bufs=1))
-        finish(MT - 2, *parts[MT - 2])
-        finish_on_vector(MT - 1, day, lamp)
+        for m in range(MT):
+            finish(m, *pick_pairs(m, scores(m)))

@@ -255,8 +255,17 @@ def tile_list_iris_blank_match_kernel(
             nc.scalar.activation(out=above[:], in_=gap[:], func=ACT.Relu)
             return gap, day_part, above
 
+        def finish_shared(m, gap, day_part, above):
+            gap_part = ring.tile([P, PAIRS], F32, name="gap_part")
+            nc.scalar.activation(out=gap_part[:], in_=gap[:], func=ACT.Copy, scale=neg_cb[:, m : m + 1])
+            partial = ring.tile([P, PAIRS], F32, name="partial", bufs=2)
+            nc.vector.scalar_tensor_tensor(partial[:], above[:], one_cb[:, m : m + 1], day_part[:], ALU.mult, ALU.add)
+            result = ring.tile([P, PAIRS], F32, name="result")
+            nc.gpsimd.tensor_tensor(result[:], partial[:], gap_part[:], ALU.add)
+            nc.sync.dma_start(out=out[P * m : P * (m + 1), :], in_=result[:])
+
         def finish(m, gap, day_part, above):
-            linear = ring.tile([P, PAIRS], F32, name="linear", bufs=2)
+            linear = ring.tile([P, PAIRS], F32, name="partial", bufs=2)
             nc.vector.scalar_tensor_tensor(linear[:], gap[:], neg_cb[:, m : m + 1], day_part[:], ALU.mult, ALU.add)
             result = ring.tile([P, PAIRS], F32, name="result")
             width = PAIRS // 2 if m == MT - 1 else PAIRS
@@ -268,4 +277,8 @@ def tile_list_iris_blank_match_kernel(
                 nc.sync.dma_start(out=out[P * m : P * (m + 1), cols], in_=result[:, cols])
 
         for m in range(MT):
-            finish(m, *pick_pairs(m, scores(m)))
+            parts = pick_pairs(m, scores(m))
+            if m < MT - 2:
+                finish_shared(m, *parts)
+            else:
+                finish(m, *parts)

@@ -16,14 +16,25 @@ ALU = mybir.AluOpType
 
 P = 128
 K, H, T, S, S2, PAIRS = 1536, 512, 4096, 1024, 1024, 512
-PASSES = K // 512
+PACK = 4
+K_PASS = P * PACK
+PASSES = K // K_PASS
 JT = S // P
 MT = S2 // P
 BANK = 512
 QUADS = 4
+ROWS_Q = 4
+PER_COLUMN = 16
+
+SCALE_AT = 64
+SCALE_END = SCALE_AT + PASSES * QUADS * ROWS_Q
 COPIED = 6
+TURN_BANK = 2
+SCORE_BANKS = (5, 0)
 E_SLOTS = 4
-LAMP_SLOTS = 4
+W1_BYTES = PACK * 4
+TAB0_AT = 6144
+SHARED = MT - 2
 
 FLOPS = 2 * (2 * K * H * S + H * S2 * S)
 
@@ -43,26 +54,32 @@ def tile_list_iris_blank_match_kernel(
         def bank(b, shape):
             return psum.tile(shape, F32, name="bank%d" % b, tag="bank%d" % b)
 
-        offs_t = lists.tile([P, S // 16], U16, name="offs_t")
-        offs2_t = lists.tile([P, S2 // 16], U16, name="offs2_t")
-        pos1_t = lists.tile([P, PAIRS // 16], U16, name="pos1_t")
-        pos2_t = lists.tile([P, PAIRS // 16], U16, name="pos2_t")
+        offs_t = lists.tile([P, S // PER_COLUMN], U16, name="offs_t")
+        offs2_t = lists.tile([P, S2 // PER_COLUMN], U16, name="offs2_t")
+        pos1_t = lists.tile([P, PAIRS // PER_COLUMN], U16, name="pos1_t")
+        pos2_t = lists.tile([P, PAIRS // PER_COLUMN], U16, name="pos2_t")
 
         def slot(shape, dtype, name, tag):
             return keep.tile(shape, dtype, name=name, tag=tag, align_bytes=64)
 
-        tab_w = [shared.tile([P, T], U32, name="tab_w0", offset=6144), slot([P, T], U32, "tab_w1", "wide1")]
+        def entries(positions, lo, hi):
+            return positions[:, lo // PER_COLUMN : hi // PER_COLUMN]
+
+        def scale_rows(tile, q):
+            return tile[32 * q : 32 * q + ROWS_Q]
+
+        tab_w = [shared.tile([P, T], U32, name="tab_w0", offset=TAB0_AT), slot([P, T], U32, "tab_w1", "wide1")]
         tab_s = slot([P, T], U8, "tab_s", "wide2")
         tab2_s = keep.tile([P, T], U8, name="tab2_s")
         w4_w = keep.tile([P, PASSES, 2 * H], U8, name="w4_w", align_bytes=64)
         w4_s = keep.tile([P, PASSES, H], U8, name="w4_s", align_bytes=64)
         v_s = keep.tile([P, PASSES, S], U8, name="v_s", align_bytes=64)
         v2_s = keep.tile([P, S2], U8, name="v2_s", align_bytes=64)
-        rows = keep.tile([P, P], F32, name="rows")
+        ex_cb_rows = keep.tile([P, P], F32, name="ex_cb_rows")
         ident = keep.tile([P, P], F32, name="ident")
 
         nc.vector.memset(w4_s[:].rearrange("p a n -> p (a n)").bitcast(I32), 0)
-        nc.vector.memset(rows[:], 0.0)
+        nc.vector.memset(ex_cb_rows[:], 0.0)
         nc.vector.memset(tab_s[:].bitcast(I32), 0)
         nc.vector.memset(tab2_s[:].bitcast(I32), 0)
         nc.vector.memset(v_s[:].rearrange("p a n -> p (a n)").bitcast(I32), 0)
@@ -74,23 +91,23 @@ def tile_list_iris_blank_match_kernel(
         tab_s_in = keep.tile([P, T // 4], I32, name="tab_s_in")
         nc.sync.dma_start(offs_t[:], offs)
         for a in range(PASSES):
-            nc.sync.dma_start(out=tab_s_in[64 + a : 112 : 3, :], in_=tab_scales[a].bitcast(I32))
+            nc.sync.dma_start(out=tab_s_in[SCALE_AT + a : SCALE_END : PASSES, :], in_=tab_scales[a].bitcast(I32))
         load_words(tab_w[0], tab_words[0])
         nc.sync.dma_start(offs2_t[:], offs2)
         nc.sync.dma_start(pos1_t[:], pos1)
         tab2_s_in = keep.tile([P, T // 4], I32, name="tab2_s_in")
-        nc.sync.dma_start(out=tab2_s_in[0:16, :], in_=tab2_scales[0].bitcast(I32))
+        nc.sync.dma_start(out=tab2_s_in[0 : QUADS * ROWS_Q, :], in_=tab2_scales[0].bitcast(I32))
         load_words(tab_w[1], tab_words[1])
         nc.sync.dma_start(out=w4_w[:].bitcast(I32), in_=w4_words.rearrange("a p n -> p a n").bitcast(I32))
         nc.sync.dma_start(pos2_t[:], pos2)
 
         for q in range(QUADS):
             nc.gpsimd.dma_start(
-                out=w4_s[32 * q : 32 * q + 4, :, :].bitcast(I32),
-                in_=w4_scales[:, 4 * q : 4 * q + 4, :].rearrange("a r n -> r a n").bitcast(I32),
+                out=scale_rows(w4_s, q).bitcast(I32),
+                in_=w4_scales[:, ROWS_Q * q : ROWS_Q * (q + 1), :].rearrange("a s n -> s a n").bitcast(I32),
             )
-        nc.gpsimd.dma_start(out=rows[0:JT, :], in_=ex.rearrange("(t p) -> t p", p=P))
-        nc.gpsimd.dma_start(out=rows[JT : JT + MT, :], in_=cb.rearrange("(t p) -> t p", p=P))
+        nc.gpsimd.dma_start(out=ex_cb_rows[0:JT, :], in_=ex.rearrange("(t p) -> t p", p=P))
+        nc.gpsimd.dma_start(out=ex_cb_rows[JT : JT + MT, :], in_=cb.rearrange("(t p) -> t p", p=P))
 
         make_identity(nc, ident[:])
 
@@ -98,12 +115,13 @@ def tile_list_iris_blank_match_kernel(
         v_s_picked = keep.tile([P, S], U8, name="v_s_picked")
         v2_s_picked = keep.tile([P, S2], U8, name="v2_s_picked")
 
-        nc.vector.tensor_copy(tab_s[64:112, :].bitcast(I32), tab_s_in[64:112, :])
+        nc.vector.tensor_copy(tab_s[SCALE_AT:SCALE_END, :].bitcast(I32), tab_s_in[SCALE_AT:SCALE_END, :])
         nc.vector.tensor_copy(v_s_picked[:], tab_s[:].indirect(offs_t[:]))
+        per_quad = PASSES * ROWS_Q
         for q in range(QUADS):
             nc.sync.dma_start(
-                out=v_s[32 * q : 32 * q + 4, :, :].bitcast(I32),
-                in_=v_s_picked[64 + 12 * q : 64 + 12 * (q + 1), :].bitcast(I32),
+                out=scale_rows(v_s, q).bitcast(I32),
+                in_=v_s_picked[SCALE_AT + per_quad * q : SCALE_AT + per_quad * (q + 1), :].bitcast(I32),
             )
         tab_w.append(slot([P, T], U32, "tab_w2", "wide2"))
         load_words(tab_w[2], tab_words[2])
@@ -112,25 +130,26 @@ def tile_list_iris_blank_match_kernel(
         w1_pieces = [(0, 0, H), (1, 0, H), (2, 0, H // 2), (2, H // 2, H)]
         w1_raw = []
         for n, (a, lo, hi) in enumerate(w1_pieces):
-            piece = shared.tile([P, 4, hi - lo], F32, name="w1_raw%d" % n, offset=16 * (a * H + lo))
+            piece = shared.tile([P, PACK, hi - lo], F32, name="w1_raw%d" % n, offset=W1_BYTES * (a * H + lo))
             nc.sync.dma_start(
-                out=piece[:], in_=w1[512 * a : 512 * (a + 1), lo:hi].rearrange("(p i) r -> p i r", i=4)
+                out=piece[:], in_=w1[K_PASS * a : K_PASS * (a + 1), lo:hi].rearrange("(p i) r -> p i r", i=PACK)
             )
             w1_raw.append(piece)
-        nc.vector.tensor_copy(tab2_s[0:16, :].bitcast(I32), tab2_s_in[0:16, :])
+
+        nc.vector.tensor_copy(tab2_s[0 : QUADS * ROWS_Q, :].bitcast(I32), tab2_s_in[0 : QUADS * ROWS_Q, :])
         nc.vector.tensor_copy(v2_s_picked[:], tab2_s[:].indirect(offs2_t[:]))
         for q in range(QUADS):
             nc.gpsimd.dma_start(
-                out=v2_s[32 * q : 32 * q + 4, :].bitcast(I32),
-                in_=v2_s_picked[4 * q : 4 * q + 4, :].bitcast(I32),
+                out=scale_rows(v2_s, q).bitcast(I32),
+                in_=v2_s_picked[ROWS_Q * q : ROWS_Q * (q + 1), :].bitcast(I32),
             )
+
         nc.vector.tensor_copy(v_w[1][:], tab_w[1][:].indirect(offs_t[:]))
         tab2_w = slot([P, T], U32, "tab2_w", "wide1")
         load_words(tab2_w, tab2_words[0])
-        for c in range(4):
-            nc.vector.tensor_copy(
-                v_w[2][:, 256 * c : 256 * (c + 1)], tab_w[2][:].indirect(offs_t[:, 16 * c : 16 * (c + 1)])
-            )
+
+        for lo in range(0, S, 2 * P):
+            nc.vector.tensor_copy(v_w[2][:, lo : lo + 2 * P], tab_w[2][:].indirect(entries(offs_t, lo, lo + 2 * P)))
 
         def first_stage_pass(acc, t, a, words, scales):
             cols = slice(P * t, P * (t + 1))
@@ -149,96 +168,97 @@ def tile_list_iris_blank_match_kernel(
         for t in range(JT):
             for a in range(PASSES):
                 first_stage_pass(acc4[t], t, a, w4_w[:, a, :].bitcast(FP4X4), w4_s[:, a, :])
-        second = [slot([P, H], F32, "second%d" % t, "second%d" % t) for t in range(COPIED)]
+        prod4 = [slot([P, H], F32, "prod4_%d" % t, "prod4_%d" % t) for t in range(COPIED)]
         for t in range(COPIED):
-            nc.scalar.copy(out=as_pairs(second[t]), in_=by_pairs(acc4[t]))
+            nc.scalar.copy(out=as_pairs(prod4[t]), in_=by_pairs(acc4[t]))
 
         turned = bank(0, [P, P])
-        nc.tensor.transpose(turned[:], rows[:], ident[:])
-        columns = keep.tile([P, JT + MT], F32, name="columns")
-        nc.scalar.copy(out=columns[:], in_=turned[:, 0 : JT + MT])
+        nc.tensor.transpose(turned[:], ex_cb_rows[:], ident[:])
+        ex_cb = keep.tile([P, JT + MT], F32, name="ex_cb")
+        nc.scalar.copy(out=ex_cb[:], in_=turned[:, 0 : JT + MT])
 
         def from_cb(name, factor, shift):
             made = keep.tile([P, MT], F32, name=name)
-            nc.gpsimd.tensor_scalar(made[:], columns[:, JT : JT + MT], factor, shift, ALU.mult, ALU.add)
+            nc.gpsimd.tensor_scalar(made[:], ex_cb[:, JT : JT + MT], factor, shift, ALU.mult, ALU.add)
             return made
 
         neg_cb = from_cb("neg_cb", -1.0, 0.0)
-        one_cb = from_cb("one_cb", 1.0, 1.0)
+        one_plus_cb = from_cb("one_plus_cb", 1.0, 1.0)
         one_minus_cb = from_cb("one_minus_cb", -1.0, 1.0)
 
         w1_w = [keep.tile([P, H], U32, name="w1_w%d" % a, align_bytes=64) for a in range(PASSES)]
         w1_s = [keep.tile([P, H], U8, name="w1_s%d" % a, align_bytes=64) for a in range(PASSES)]
-        w1_bf = slot([P, PASSES, 4 * H], BF16, "w1_bf", "wide2")
+        w1_bf = slot([P, PASSES, PACK * H], BF16, "w1_bf", "wide2")
         for piece, (a, lo, hi) in zip(w1_raw, w1_pieces):
-            rounded = w1_bf[:, a, 4 * lo : 4 * hi]
+            rounded = w1_bf[:, a, PACK * lo : PACK * hi]
             nc.vector.tensor_copy(
-                out=rounded.rearrange("p (c n i) -> p c i n", n=4, i=4),
+                out=rounded.rearrange("p (c n i) -> p c i n", n=4, i=PACK),
                 in_=piece[:].rearrange("p i (c n) -> p c i n", n=4),
             )
             nc.vector.quantize_mx(out=w1_w[a][:, lo:hi].bitcast(FP8X4), scales=w1_s[a][:, lo:hi], in_=rounded)
 
-        def first_product(t):
+        def w1_product(t):
             acc = bank(t % COPIED, [P, BANK])
             for a in range(PASSES):
                 first_stage_pass(acc, t, a, w1_w[a][:].bitcast(FP8X4), w1_s[a][:])
             return acc
 
-        acc1 = [first_product(t) for t in range(COPIED)]
+        acc1 = [w1_product(t) for t in range(COPIED)]
 
         h_w = keep.tile([P, S], U32, name="h_w", align_bytes=64)
         h_s = keep.tile([P, S], U8, name="h_s", align_bytes=64)
 
         def make_h(t):
-            acc = acc1[t] if t < COPIED else first_product(t)
+            acc = acc1[t] if t < COPIED else w1_product(t)
             tone = slot([P, H], F32, "tone", "tone%d" % t)
-            nc.scalar.activation(out=as_pairs(tone), in_=by_pairs(acc), func=ACT.Tanh, bias=columns[:, t : t + 1])
+            nc.scalar.activation(out=as_pairs(tone), in_=by_pairs(acc), func=ACT.Tanh, bias=ex_cb[:, t : t + 1])
             h_t = ring.tile([P, H], BF16, name="h_t", bufs=4)
             if t < COPIED:
-                nc.vector.tensor_tensor(h_t[:], tone[:], second[t][:], ALU.mult)
+                nc.vector.tensor_tensor(h_t[:], tone[:], prod4[t][:], ALU.mult)
             else:
                 nc.vector.tensor_tensor(as_pairs(h_t), as_pairs(tone), by_pairs(acc4[t]), ALU.mult)
             return h_t
 
         def turn_and_quantise(g, h_pair):
-            xt = bank(2 + g, [P, 2, 2, P])
+            h_turned = bank(TURN_BANK + g, [P, 2, 2, P])
             for t in range(2):
                 words = h_pair[t][:].bitcast(F32)
                 for u in range(2):
-                    nc.tensor.transpose(xt[:, t, u, :], words[:, P * u : P * (u + 1)], ident[:])
-            h_bf = ring.tile([P, 4 * 2 * P], BF16, name="h_bf", align_bytes=64)
+                    nc.tensor.transpose(h_turned[:, t, u, :], words[:, P * u : P * (u + 1)], ident[:])
+            h_bf = ring.tile([P, PACK * 2 * P], BF16, name="h_bf", align_bytes=64)
             nc.scalar.copy(
                 out=h_bf[:].bitcast(F32).rearrange("p (t j u) -> p t j u", t=2, u=2),
-                in_=xt[:].rearrange("p t u j -> p t j u"),
+                in_=h_turned[:].rearrange("p t u j -> p t j u"),
             )
             cols = slice(2 * P * g, 2 * P * (g + 1))
             nc.vector.quantize_mx(out=h_w[:, cols].bitcast(FP8X4), scales=h_s[:, cols], in_=h_bf[:])
 
-        def gather_candidates(c, tag):
-            half = slot([P, S2 // 2], U32, "v2_w%d" % c, tag)
-            nc.vector.tensor_copy(half[:], tab2_w[:].indirect(offs2_t[:, 32 * c : 32 * (c + 1)]))
+        def gather_blanks(c, after):
+            half = slot([P, S2 // 2], U32, "v2_w%d" % c, "tone%d" % after)
+            nc.vector.tensor_copy(half[:], tab2_w[:].indirect(entries(offs2_t, S2 // 2 * c, S2 // 2 * (c + 1))))
             return half
 
         v2_w = []
         h_tiles = [make_h(0), make_h(1)]
         for g in range(JT // 2):
             if g == 1:
-                v2_w.append(gather_candidates(0, "tone1"))
-            if g == 3:
-                v2_w.append(gather_candidates(1, "tone7"))
+                v2_w.append(gather_blanks(0, 1))
             if g + 1 < JT // 2:
                 h_tiles.extend([make_h(2 * g + 2), make_h(2 * g + 3)])
+            else:
+                v2_w.append(gather_blanks(1, JT - 1))
             turn_and_quantise(g, h_tiles[2 * g : 2 * g + 2])
 
         def scores(m):
             e = slot([P, S], F32, "e", "e%d" % (m % E_SLOTS))
-            rows_m = slice(P * m, P * (m + 1))
-            width = BANK // 2 if m == 0 else BANK
+            half, place = divmod(m, MT // 2)
+            width = 2 * P if m == 0 else BANK
             for c in range(S // width):
                 cols = slice(width * c, width * (c + 1))
-                acc = bank(2 + c if m == 0 else (5, 0)[c], [P, width])
+                acc = bank(TURN_BANK + c if m == 0 else SCORE_BANKS[c], [P, width])
                 nc.tensor.matmul_mx(
-                    out=acc[:], lhsT=v2_w[m // 4][:, P * (m % 4) : P * (m % 4 + 1)].bitcast(FP8X4), lhsT_scale=v2_s[:, rows_m],
+                    out=acc[:], lhsT=v2_w[half][:, P * place : P * (place + 1)].bitcast(FP8X4),
+                    lhsT_scale=v2_s[:, P * m : P * (m + 1)],
                     rhs=h_w[:, cols].bitcast(FP8X4), rhs_scale=h_s[:, cols], start=True, stop=True,
                 )
                 nc.scalar.copy(out=e[:, cols], in_=acc[:])
@@ -259,26 +279,31 @@ def tile_list_iris_blank_match_kernel(
             gap_part = ring.tile([P, PAIRS], F32, name="gap_part")
             nc.scalar.activation(out=gap_part[:], in_=gap[:], func=ACT.Copy, scale=neg_cb[:, m : m + 1])
             partial = ring.tile([P, PAIRS], F32, name="partial", bufs=2)
-            nc.vector.scalar_tensor_tensor(partial[:], above[:], one_cb[:, m : m + 1], day_part[:], ALU.mult, ALU.add)
+            nc.vector.scalar_tensor_tensor(
+                partial[:], above[:], one_plus_cb[:, m : m + 1], day_part[:], ALU.mult, ALU.add
+            )
             result = ring.tile([P, PAIRS], F32, name="result")
             nc.gpsimd.tensor_tensor(result[:], partial[:], gap_part[:], ALU.add)
             nc.sync.dma_start(out=out[P * m : P * (m + 1), :], in_=result[:])
 
-        def finish(m, gap, day_part, above):
-            linear = ring.tile([P, PAIRS], F32, name="partial", bufs=2)
-            nc.vector.scalar_tensor_tensor(linear[:], gap[:], neg_cb[:, m : m + 1], day_part[:], ALU.mult, ALU.add)
+        def finish_on_vector(m, gap, day_part, above):
+            partial = ring.tile([P, PAIRS], F32, name="partial", bufs=2)
+            nc.vector.scalar_tensor_tensor(partial[:], gap[:], neg_cb[:, m : m + 1], day_part[:], ALU.mult, ALU.add)
             result = ring.tile([P, PAIRS], F32, name="result")
             width = PAIRS // 2 if m == MT - 1 else PAIRS
             for lo in range(0, PAIRS, width):
                 cols = slice(lo, lo + width)
                 nc.vector.scalar_tensor_tensor(
-                    result[:, cols], above[:, cols], one_cb[:, m : m + 1], linear[:, cols], ALU.mult, ALU.add
+                    result[:, cols], above[:, cols], one_plus_cb[:, m : m + 1], partial[:, cols], ALU.mult, ALU.add
                 )
                 nc.sync.dma_start(out=out[P * m : P * (m + 1), cols], in_=result[:, cols])
 
+        e_tiles = [scores(0)]
         for m in range(MT):
-            parts = pick_pairs(m, scores(m))
-            if m < MT - 2:
+            if m + 1 < MT:
+                e_tiles.append(scores(m + 1))
+            parts = pick_pairs(m, e_tiles[m])
+            if m < SHARED:
                 finish_shared(m, *parts)
             else:
-                finish(m, *parts)
+                finish_on_vector(m, *parts)

from contextlib import ExitStack

import concourse.mybir as mybir
from concourse.masks import make_identity

F32 = mybir.dt.float32
BF16 = mybir.dt.bfloat16
I32 = mybir.dt.int32
U32 = mybir.dt.uint32
U16 = mybir.dt.uint16
U8 = mybir.dt.uint8
FP8X4 = mybir.dt.float8_e4m3fn_x4
FP4X4 = mybir.dt.float4_e2m1fn_x4
ACT = mybir.ActivationFunctionType
ALU = mybir.AluOpType

P = 128
K, H, T, S, S2, PAIRS = 1536, 512, 4096, 1024, 1024, 512
PACK = 4
K_PASS = P * PACK
PASSES = K // K_PASS
JT = S // P
MT = S2 // P
BANK = 512
QUADS = 4
ROWS_Q = 4
PER_COLUMN = 16

SCALE_AT = 64
SCALE_END = SCALE_AT + PASSES * QUADS * ROWS_Q
COPIED = 6
TURN_BANK = 2
SCORE_BANKS = (5, 0)
E_SLOTS = 4
W1_BYTES = PACK * 4
TAB0_AT = 6144
SHARED = MT - 2

FLOPS = 2 * (2 * K * H * S + H * S2 * S)


def tile_list_iris_blank_match_kernel(
    tc, tab_words, tab_scales, tab2_words, tab2_scales, offs, offs2, pos1, pos2,
    w1, w4_words, w4_scales, ex, cb, out,
):
    nc = tc.nc
    with ExitStack() as ctx:
        lists = ctx.enter_context(tc.tile_pool(name="lists", bufs=1))
        keep = ctx.enter_context(tc.tile_pool(name="keep", bufs=1))
        shared = ctx.enter_context(tc.tile_pool(name="shared", bufs=1))
        ring = ctx.enter_context(tc.tile_pool(name="ring", bufs=3))
        psum = ctx.enter_context(tc.psum_pool(name="psum", bufs=1))

        def bank(b, shape):
            return psum.tile(shape, F32, name="bank%d" % b, tag="bank%d" % b)

        offs_t = lists.tile([P, S // PER_COLUMN], U16, name="offs_t")
        offs2_t = lists.tile([P, S2 // PER_COLUMN], U16, name="offs2_t")
        pos1_t = lists.tile([P, PAIRS // PER_COLUMN], U16, name="pos1_t")
        pos2_t = lists.tile([P, PAIRS // PER_COLUMN], U16, name="pos2_t")

        def slot(shape, dtype, name, tag):
            return keep.tile(shape, dtype, name=name, tag=tag, align_bytes=64)

        def entries(positions, lo, hi):
            return positions[:, lo // PER_COLUMN : hi // PER_COLUMN]

        def scale_rows(tile, q):
            return tile[32 * q : 32 * q + ROWS_Q]

        tab_w = [shared.tile([P, T], U32, name="tab_w0", offset=TAB0_AT), slot([P, T], U32, "tab_w1", "wide1")]
        tab_s = slot([P, T], U8, "tab_s", "wide2")
        tab2_s = keep.tile([P, T], U8, name="tab2_s")
        w4_w = keep.tile([P, PASSES, 2 * H], U8, name="w4_w", align_bytes=64)
        w4_s = keep.tile([P, PASSES, H], U8, name="w4_s", align_bytes=64)
        v_s = keep.tile([P, PASSES, S], U8, name="v_s", align_bytes=64)
        v2_s = keep.tile([P, S2], U8, name="v2_s", align_bytes=64)
        ex_cb_rows = keep.tile([P, P], F32, name="ex_cb_rows")
        ident = keep.tile([P, P], F32, name="ident")

        nc.vector.memset(w4_s[:].rearrange("p a n -> p (a n)").bitcast(I32), 0)
        nc.vector.memset(ex_cb_rows[:], 0.0)
        nc.vector.memset(tab_s[:].bitcast(I32), 0)
        nc.vector.memset(tab2_s[:].bitcast(I32), 0)
        nc.vector.memset(v_s[:].rearrange("p a n -> p (a n)").bitcast(I32), 0)
        nc.vector.memset(v2_s[:].bitcast(I32), 0)

        def load_words(dst, src):
            nc.sync.dma_start(out=dst[:].bitcast(I32), in_=src.rearrange("p t i -> p (t i)").bitcast(I32))

        tab_s_in = keep.tile([P, T // 4], I32, name="tab_s_in")
        nc.sync.dma_start(offs_t[:], offs)
        for a in range(PASSES):
            nc.sync.dma_start(out=tab_s_in[SCALE_AT + a : SCALE_END : PASSES, :], in_=tab_scales[a].bitcast(I32))
        load_words(tab_w[0], tab_words[0])
        nc.sync.dma_start(offs2_t[:], offs2)
        nc.sync.dma_start(pos1_t[:], pos1)
        tab2_s_in = keep.tile([P, T // 4], I32, name="tab2_s_in")
        nc.sync.dma_start(out=tab2_s_in[0 : QUADS * ROWS_Q, :], in_=tab2_scales[0].bitcast(I32))
        load_words(tab_w[1], tab_words[1])
        nc.sync.dma_start(out=w4_w[:].bitcast(I32), in_=w4_words.rearrange("a p n -> p a n").bitcast(I32))
        nc.sync.dma_start(pos2_t[:], pos2)

        for q in range(QUADS):
            nc.gpsimd.dma_start(
                out=scale_rows(w4_s, q).bitcast(I32),
                in_=w4_scales[:, ROWS_Q * q : ROWS_Q * (q + 1), :].rearrange("a s n -> s a n").bitcast(I32),
            )
        nc.gpsimd.dma_start(out=ex_cb_rows[0:JT, :], in_=ex.rearrange("(t p) -> t p", p=P))
        nc.gpsimd.dma_start(out=ex_cb_rows[JT : JT + MT, :], in_=cb.rearrange("(t p) -> t p", p=P))

        make_identity(nc, ident[:])

        v_w = [keep.tile([P, S], U32, name="v_w%d" % a, align_bytes=64) for a in range(PASSES)]
        v_s_picked = keep.tile([P, S], U8, name="v_s_picked")
        v2_s_picked = keep.tile([P, S2], U8, name="v2_s_picked")

        nc.vector.tensor_copy(tab_s[SCALE_AT:SCALE_END, :].bitcast(I32), tab_s_in[SCALE_AT:SCALE_END, :])
        nc.vector.tensor_copy(v_s_picked[:], tab_s[:].indirect(offs_t[:]))
        per_quad = PASSES * ROWS_Q
        for q in range(QUADS):
            nc.sync.dma_start(
                out=scale_rows(v_s, q).bitcast(I32),
                in_=v_s_picked[SCALE_AT + per_quad * q : SCALE_AT + per_quad * (q + 1), :].bitcast(I32),
            )
        tab_w.append(slot([P, T], U32, "tab_w2", "wide2"))
        load_words(tab_w[2], tab_words[2])

        nc.vector.tensor_copy(v_w[0][:], tab_w[0][:].indirect(offs_t[:]))
        w1_pieces = [(0, 0, H), (1, 0, H), (2, 0, H // 2), (2, H // 2, H)]
        w1_raw = []
        for n, (a, lo, hi) in enumerate(w1_pieces):
            piece = shared.tile([P, PACK, hi - lo], F32, name="w1_raw%d" % n, offset=W1_BYTES * (a * H + lo))
            nc.sync.dma_start(
                out=piece[:], in_=w1[K_PASS * a : K_PASS * (a + 1), lo:hi].rearrange("(p i) r -> p i r", i=PACK)
            )
            w1_raw.append(piece)

        nc.vector.tensor_copy(tab2_s[0 : QUADS * ROWS_Q, :].bitcast(I32), tab2_s_in[0 : QUADS * ROWS_Q, :])
        nc.vector.tensor_copy(v2_s_picked[:], tab2_s[:].indirect(offs2_t[:]))
        for q in range(QUADS):
            nc.gpsimd.dma_start(
                out=scale_rows(v2_s, q).bitcast(I32),
                in_=v2_s_picked[ROWS_Q * q : ROWS_Q * (q + 1), :].bitcast(I32),
            )

        nc.vector.tensor_copy(v_w[1][:], tab_w[1][:].indirect(offs_t[:]))
        tab2_w = slot([P, T], U32, "tab2_w", "wide1")
        load_words(tab2_w, tab2_words[0])

        for lo in range(0, S, 2 * P):
            nc.vector.tensor_copy(v_w[2][:, lo : lo + 2 * P], tab_w[2][:].indirect(entries(offs_t, lo, lo + 2 * P)))

        def first_stage_pass(acc, t, a, words, scales):
            cols = slice(P * t, P * (t + 1))
            nc.tensor.matmul_mx(
                out=acc[:], lhsT=v_w[a][:, cols].bitcast(FP8X4), lhsT_scale=v_s[:, a, cols],
                rhs=words, rhs_scale=scales, start=(a == 0), stop=(a == PASSES - 1),
            )

        def by_pairs(acc):
            return acc[:].rearrange("p (q u e) -> p u q e", u=2, e=2)

        def as_pairs(tile):
            return tile[:].rearrange("p (u q e) -> p u q e", u=2, e=2)

        acc4 = [bank(t, [P, BANK]) for t in range(JT)]
        for t in range(JT):
            for a in range(PASSES):
                first_stage_pass(acc4[t], t, a, w4_w[:, a, :].bitcast(FP4X4), w4_s[:, a, :])
        prod4 = [slot([P, H], F32, "prod4_%d" % t, "prod4_%d" % t) for t in range(COPIED)]
        for t in range(COPIED):
            nc.scalar.copy(out=as_pairs(prod4[t]), in_=by_pairs(acc4[t]))

        turned = bank(0, [P, P])
        nc.tensor.transpose(turned[:], ex_cb_rows[:], ident[:])
        ex_cb = keep.tile([P, JT + MT], F32, name="ex_cb")
        nc.scalar.copy(out=ex_cb[:], in_=turned[:, 0 : JT + MT])

        def from_cb(name, factor, shift):
            made = keep.tile([P, MT], F32, name=name)
            nc.gpsimd.tensor_scalar(made[:], ex_cb[:, JT : JT + MT], factor, shift, ALU.mult, ALU.add)
            return made

        neg_cb = from_cb("neg_cb", -1.0, 0.0)
        one_plus_cb = from_cb("one_plus_cb", 1.0, 1.0)
        one_minus_cb = from_cb("one_minus_cb", -1.0, 1.0)

        w1_w = [keep.tile([P, H], U32, name="w1_w%d" % a, align_bytes=64) for a in range(PASSES)]
        w1_s = [keep.tile([P, H], U8, name="w1_s%d" % a, align_bytes=64) for a in range(PASSES)]
        w1_bf = slot([P, PASSES, PACK * H], BF16, "w1_bf", "wide2")
        for piece, (a, lo, hi) in zip(w1_raw, w1_pieces):
            rounded = w1_bf[:, a, PACK * lo : PACK * hi]
            nc.vector.tensor_copy(
                out=rounded.rearrange("p (c n i) -> p c i n", n=4, i=PACK),
                in_=piece[:].rearrange("p i (c n) -> p c i n", n=4),
            )
            nc.vector.quantize_mx(out=w1_w[a][:, lo:hi].bitcast(FP8X4), scales=w1_s[a][:, lo:hi], in_=rounded)

        def w1_product(t):
            acc = bank(t % COPIED, [P, BANK])
            for a in range(PASSES):
                first_stage_pass(acc, t, a, w1_w[a][:].bitcast(FP8X4), w1_s[a][:])
            return acc

        acc1 = [w1_product(t) for t in range(COPIED)]

        h_w = keep.tile([P, S], U32, name="h_w", align_bytes=64)
        h_s = keep.tile([P, S], U8, name="h_s", align_bytes=64)

        def make_h(t):
            acc = acc1[t] if t < COPIED else w1_product(t)
            tone = slot([P, H], F32, "tone", "tone%d" % t)
            nc.scalar.activation(out=as_pairs(tone), in_=by_pairs(acc), func=ACT.Tanh, bias=ex_cb[:, t : t + 1])
            h_t = ring.tile([P, H], BF16, name="h_t", bufs=4)
            if t < COPIED:
                nc.vector.tensor_tensor(h_t[:], tone[:], prod4[t][:], ALU.mult)
            else:
                nc.vector.tensor_tensor(as_pairs(h_t), as_pairs(tone), by_pairs(acc4[t]), ALU.mult)
            return h_t

        def turn_and_quantise(g, h_pair):
            h_turned = bank(TURN_BANK + g, [P, 2, 2, P])
            for t in range(2):
                words = h_pair[t][:].bitcast(F32)
                for u in range(2):
                    nc.tensor.transpose(h_turned[:, t, u, :], words[:, P * u : P * (u + 1)], ident[:])
            h_bf = ring.tile([P, PACK * 2 * P], BF16, name="h_bf", align_bytes=64)
            nc.scalar.copy(
                out=h_bf[:].bitcast(F32).rearrange("p (t j u) -> p t j u", t=2, u=2),
                in_=h_turned[:].rearrange("p t u j -> p t j u"),
            )
            cols = slice(2 * P * g, 2 * P * (g + 1))
            nc.vector.quantize_mx(out=h_w[:, cols].bitcast(FP8X4), scales=h_s[:, cols], in_=h_bf[:])

        def gather_blanks(c, after):
            half = slot([P, S2 // 2], U32, "v2_w%d" % c, "tone%d" % after)
            nc.vector.tensor_copy(half[:], tab2_w[:].indirect(entries(offs2_t, S2 // 2 * c, S2 // 2 * (c + 1))))
            return half

        v2_w = []
        h_tiles = [make_h(0), make_h(1)]
        for g in range(JT // 2):
            if g == 1:
                v2_w.append(gather_blanks(0, 1))
            if g + 1 < JT // 2:
                h_tiles.extend([make_h(2 * g + 2), make_h(2 * g + 3)])
            else:
                v2_w.append(gather_blanks(1, JT - 1))
            turn_and_quantise(g, h_tiles[2 * g : 2 * g + 2])

        def scores(m):
            e = slot([P, S], F32, "e", "e%d" % (m % E_SLOTS))
            half, place = divmod(m, MT // 2)
            width = 2 * P if m == 0 else BANK
            for c in range(S // width):
                cols = slice(width * c, width * (c + 1))
                acc = bank(TURN_BANK + c if m == 0 else SCORE_BANKS[c], [P, width])
                nc.tensor.matmul_mx(
                    out=acc[:], lhsT=v2_w[half][:, P * place : P * (place + 1)].bitcast(FP8X4),
                    lhsT_scale=v2_s[:, P * m : P * (m + 1)],
                    rhs=h_w[:, cols].bitcast(FP8X4), rhs_scale=h_s[:, cols], start=True, stop=True,
                )
                nc.scalar.copy(out=e[:, cols], in_=acc[:])
            return e

        def pick_pairs(m, e):
            day = ring.tile([P, PAIRS], F32, name="day")
            nc.vector.tensor_copy(day[:], e[:].indirect(pos1_t[:]))
            gap = ring.tile([P, PAIRS], F32, name="gap")
            nc.vector.tensor_tensor(gap[:], e[:].indirect(pos2_t[:]), day[:], ALU.subtract)
            day_part = ring.tile([P, PAIRS], F32, name="day_part")
            nc.scalar.activation(out=day_part[:], in_=day[:], func=ACT.Copy, scale=one_minus_cb[:, m : m + 1])
            above = ring.tile([P, PAIRS], F32, name="above")
            nc.scalar.activation(out=above[:], in_=gap[:], func=ACT.Relu)
            return gap, day_part, above

        def finish_shared(m, gap, day_part, above):
            gap_part = ring.tile([P, PAIRS], F32, name="gap_part")
            nc.scalar.activation(out=gap_part[:], in_=gap[:], func=ACT.Copy, scale=neg_cb[:, m : m + 1])
            partial = ring.tile([P, PAIRS], F32, name="partial", bufs=2)
            nc.vector.scalar_tensor_tensor(
                partial[:], above[:], one_plus_cb[:, m : m + 1], day_part[:], ALU.mult, ALU.add
            )
            result = ring.tile([P, PAIRS], F32, name="result")
            nc.gpsimd.tensor_tensor(result[:], partial[:], gap_part[:], ALU.add)
            nc.sync.dma_start(out=out[P * m : P * (m + 1), :], in_=result[:])

        def finish_on_vector(m, gap, day_part, above):
            partial = ring.tile([P, PAIRS], F32, name="partial", bufs=2)
            nc.vector.scalar_tensor_tensor(partial[:], gap[:], neg_cb[:, m : m + 1], day_part[:], ALU.mult, ALU.add)
            result = ring.tile([P, PAIRS], F32, name="result")
            width = PAIRS // 2 if m == MT - 1 else PAIRS
            for lo in range(0, PAIRS, width):
                cols = slice(lo, lo + width)
                nc.vector.scalar_tensor_tensor(
                    result[:, cols], above[:, cols], one_plus_cb[:, m : m + 1], partial[:, cols], ALU.mult, ALU.add
                )
                nc.sync.dma_start(out=out[P * m : P * (m + 1), cols], in_=result[:, cols])

        e_tiles = [scores(0)]
        for m in range(MT):
            if m + 1 < MT:
                e_tiles.append(scores(m + 1))
            parts = pick_pairs(m, e_tiles[m])
            if m < SHARED:
                finish_shared(m, *parts)
            else:
                finish_on_vector(m, *parts)
